import numpy as np
import ml_dtypes


def mxq(x, axis, fmt="e4m3"):
    dtype, down = {"e4m3": (ml_dtypes.float8_e4m3fn, 7), "e5m2": (ml_dtypes.float8_e5m2, 14)}[fmt]
    v = np.moveaxis(np.asarray(x, np.float32).astype(ml_dtypes.bfloat16).astype(np.float64), axis, -1)
    blocks = v.reshape(v.shape[:-1] + (-1, 32))
    amax = np.abs(blocks).max(-1, keepdims=True)
    byte = np.maximum(np.where(amax > 0, np.frexp(amax)[1] - 1 + 127, 0) - down, 1)
    scale = np.exp2(byte - 127.0)
    codes = (blocks / scale).astype(np.float32).astype(dtype).astype(np.float64)
    return np.moveaxis((codes * scale).reshape(v.shape), -1, axis)


WIDE = False


def mx_kscale(k):
    if not WIDE:
        return np.ones(k)
    levels = np.array([10, -10, 5, -5, 0])
    if k % 512:
        return np.exp2(np.random.permutation(np.resize(levels, k // 32))).repeat(32)
    a = np.empty((k // 512, 16))
    for p in range(k // 512):
        a[p, :8] = np.random.permutation(np.resize(levels, 8))
        for g in range(8):
            far = levels[np.abs(levels - a[p, g]) >= 10]
            a[p, g + 8] = far[np.random.randint(len(far))]
    return np.exp2(a.ravel()).repeat(32)


def f64(x):
    return np.asarray(x).astype(np.float64)


def striped(idx):
    return np.tile(idx.reshape(-1, 16).T, (8, 1)).astype(np.uint16)


def unstriped(offs):
    return offs[:16].T.reshape(-1).astype(np.int64)


E2M1 = np.array([0.0, 0.5, 1.0, 1.5, 2.0, 3.0, 4.0, 6.0, -0.0, -0.5, -1.0, -1.5, -2.0, -3.0, -4.0, -6.0])


def pack_weight(w, fmt):
    k, n = w.shape
    w = f64(np.asarray(w, np.float32).astype(ml_dtypes.bfloat16)).reshape(k // 32, 32, n)
    amax = np.abs(w).max(1)
    if fmt == "e4m3":
        byte = np.frexp(amax)[1] - 1 + 127 - 7
    else:
        mant, ex = np.frexp(amax / 6.0)
        byte = np.where(mant > 0.5, ex, ex - 1) + 127
    byte = np.clip(np.where(amax > 0, byte, 1), 1, 254)
    scaled = (w * np.exp2(127.0 - byte)[:, None, :]).reshape(k, n).astype(np.float32)
    by_word = np.ascontiguousarray(scaled.reshape(k // 512, 128, 4, n).transpose(0, 1, 3, 2))
    if fmt == "e4m3":
        words = by_word.astype(ml_dtypes.float8_e4m3fn).view(np.uint8)
    else:
        c = by_word.astype(ml_dtypes.float4_e2m1fn).view(np.uint8) & 0xF
        words = (c[..., 0::2] | (c[..., 1::2] << 4)).reshape(k // 512, 128, 2 * n)
    return np.ascontiguousarray(words), np.ascontiguousarray(byte.astype(np.uint8).reshape(k // 512, 16, n))


def unpack_weight(words, scales, fmt):
    g, _, n = scales.shape
    words = np.ascontiguousarray(words).reshape(g, 128, n, -1)
    if fmt == "e4m3":
        vals = words.view(ml_dtypes.float8_e4m3fn).astype(np.float64)
    else:
        nib = np.empty((g, 128, n, 4), np.uint8)
        nib[..., 0::2] = words & 0xF
        nib[..., 1::2] = words >> 4
        vals = E2M1[nib]
    vals = vals * np.repeat(np.exp2(scales.astype(np.float64) - 127.0), 8, axis=1)[..., None]
    return vals.transpose(0, 1, 3, 2).reshape(g * 512, n)


def gelu(v):
    return 0.5 * v * (1.0 + np.tanh(np.sqrt(2.0 / np.pi) * (v + 0.044715 * v**3)))


def striped8(idx):
    return np.concatenate([v.reshape(-1, 16).T for v in idx]).astype(np.uint16)


def unstriped8(offs):
    return np.stack([offs[16 * g:16 * g + 16].T.reshape(-1) for g in range(8)]).astype(np.int64)


def put_heads(h, wgs, idx8, t2):
    r = np.arange(h.shape[0])
    page = np.zeros((h.shape[0], t2))
    page[r[:, None], idx8[r % 512 // 64]] = wgs[r // 4 % 128] * h
    return page


K, T, S, T2, H, N = 1024, 2048, 1024, 2048, 1024, 512

def setup_inputs():
    n = np.random.standard_normal
    s = mx_kscale(K)[:, None]
    u = mx_kscale(H)[:, None]
    tab_words, tab_scales = pack_weight(n((K, T)) * s, "e4m3")
    w1_words, w1_scales = pack_weight(n((K, H)) / s / np.sqrt(K), "e2m1")
    return {
        "tab_words": tab_words, "tab_scales": tab_scales,
        "offs": striped(np.random.permutation(T)[:S]),
        "w1_words": w1_words, "w1_scales": w1_scales,
        "reads": (0.8 * n((H, S))).astype(np.float32),
        "gain": (np.random.uniform(1.0, 2.5, H) * u[:, 0]).astype(np.float32),
        "offs2": striped8(np.stack([np.random.permutation(T2)[:S] for _ in range(8)])),
        "wgs": np.repeat(np.random.uniform(0.5, 2.0, (8, S)), 16, axis=0).astype(np.float32),
        "cal": (n((H, T2)) * u).astype(np.float32),
        "w2": (n((H, N)) / u / np.sqrt(H)).astype(np.float32),
    }

def reference(tab_words, tab_scales, offs, w1_words, w1_scales, reads, gain,
              offs2, wgs, cal, w2):
    v = unpack_weight(tab_words, tab_scales, "e4m3")[:, unstriped(offs)]
    w1 = unpack_weight(w1_words, w1_scales, "e2m1")
    d = (w1.T @ v) - f64(reads)
    h = d / (1.0 + d * d) * f64(gain)[:, None]
    page = put_heads(h, f64(wgs), unstriped8(offs2), T2)
    z = mxq(f64(cal) - page, 0, "e4m3")
    wq = mxq(f64(w2), 0, "e4m3")
    return wq.T @ z

@@ -1,0 +1,265 @@
+from contextlib import ExitStack
+
+import concourse.mybir as mybir
+
+K, T, S, T2, H, N = 1024, 2048, 1024, 2048, 1024, 512
+FLOPS = 2 * K * H * S + 2 * H * N * T2
+
+F32 = mybir.dt.float32
+BF16 = mybir.dt.bfloat16
+I32 = mybir.dt.int32
+U32 = mybir.dt.uint32
+U16 = mybir.dt.uint16
+U8 = mybir.dt.uint8
+FP8X4 = mybir.dt.float8_e4m3fn_x4
+FP4X4 = mybir.dt.float4_e2m1fn_x4
+ALU = mybir.AluOpType
+ACT = mybir.ActivationFunctionType
+
+P = 128
+PACK = 4
+PASSES = 2
+BANK = 512
+SLICES = PASSES * PACK
+HALF = 1024
+
+M1_ON_VECTOR = (3, 5, 7)
+TT_SCATTER = False
+Z_ON_VECTOR = ()
+
+
+def tile_list_axle_calibration_audit_kernel(
+    tc, tab_words, tab_scales, offs, w1_words, w1_scales, reads, gain, offs2, wgs, cal, w2, out
+):
+    nc = tc.nc
+    with ExitStack() as ctx:
+        keep = ctx.enter_context(tc.tile_pool(name="keep", bufs=1))
+        ring = ctx.enter_context(tc.tile_pool(name="ring", bufs=3))
+        psum = ctx.enter_context(tc.psum_pool(name="psum", bufs=1))
+
+        pick = keep.tile([P, S // 16], U16, name="pick")
+        place = keep.tile([P, S // 16], U16, name="place")
+
+        tab_sc = ring.tile([P, PASSES, T], U8, name="tab_sc", tag="narrow", align_bytes=64)
+        w1_sc_raw = ring.tile([P, PASSES, H], U8, name="w1_sc_raw", tag="narrow", align_bytes=64)
+        nc.vector.memset(tab_sc[:].bitcast(I32), 0)
+        nc.vector.memset(w1_sc_raw[:].bitcast(I32), 0)
+        nc.sync.dma_start(pick[:], offs)
+        nc.sync.dma_start(place[:], offs2)
+        gain_t = keep.tile([P, PASSES, PACK], F32, name="gain_t")
+        nc.sync.dma_start(out=gain_t[:], in_=gain.rearrange("(b p i) -> p b i", b=PASSES, i=PACK))
+        w1_raw = ring.tile([P, PASSES, 2 * H], U8, name="w1_raw", tag="wide", align_bytes=64)
+        nc.sync.dma_start(out=w1_raw[:].bitcast(I32), in_=w1_words.rearrange("a p n -> p a n").bitcast(I32))
+        tab_w = [ring.tile([P, T], I32, name=f"tab_w{a}", tag="wide", align_bytes=64) for a in range(PASSES)]
+        for a in range(PASSES):
+            nc.sync.dma_start(out=tab_w[a][:], in_=tab_words[a].rearrange("p t i -> p (t i)").bitcast(I32))
+        for q in range(4):
+            nc.scalar.dma_start(
+                out=tab_sc[32 * q : 32 * q + 4].bitcast(I32),
+                in_=tab_scales[:, 4 * q : 4 * q + 4, :].rearrange("a r n -> r a n").bitcast(I32),
+            )
+        for q in range(4):
+            nc.gpsimd.dma_start(
+                out=w1_sc_raw[32 * q : 32 * q + 4].bitcast(I32),
+                in_=w1_scales[:, 4 * q : 4 * q + 4, :].rearrange("a r n -> r a n").bitcast(I32),
+            )
+        reads_v = reads.rearrange("(b p i) j -> b i p j", b=PASSES, i=PACK)
+        cal_v = cal.rearrange("(b p i) m -> b i p m", b=PASSES, i=PACK)
+        reads_t = {}
+        cal_t = {}
+
+        def load_reads(s):
+            reads_t[s] = ring.tile([P, S], F32, name="reads_s", tag="narrow", align_bytes=64)
+            nc.sync.dma_start(out=reads_t[s][:], in_=reads_v[s // PACK, s % PACK])
+
+        def load_cal(s):
+            cal_t[s] = ring.tile([P, T2], F32, name="cal_s", tag="wide", align_bytes=64)
+            nc.sync.dma_start(out=cal_t[s][:], in_=cal_v[s // PACK, s % PACK])
+
+        load_reads(0)
+        wgs_t = keep.tile([P, S], F32, name="wgs_t")
+        nc.sync.dma_start(out=wgs_t[:], in_=wgs)
+
+        pages = [keep.tile([P, T2], F32, name=f"page{u}") for u in range(3)]
+        nc.vector.memset(pages[0][:], 0.0)
+        nc.gpsimd.memset(pages[1][:], 0.0)
+        nc.gpsimd.memset(pages[2][:], 0.0)
+
+        z_rows = [keep.tile([P, PACK * T2 // 2], F32, name=f"z_rows{b}", align_bytes=64) for b in range(PASSES)]
+        r_first = keep.tile([P, S], F32, name="r_first")
+
+        def z_plane(s):
+            b, i = divmod(s, PACK)
+            return z_rows[b][:, i * S : (i + 1) * S]
+
+        w1_c = [keep.tile([P, PASSES, PACK, 2 * P], U8, name=f"w1_c{b}", align_bytes=64) for b in range(PASSES)]
+        w1_s = [keep.tile([P, PASSES, PACK, P], U8, name=f"w1_s{b}", align_bytes=64) for b in range(PASSES)]
+
+        def order_w1(b):
+            cols = slice(b * BANK, (b + 1) * BANK)
+            nc.vector.tensor_copy(
+                out=w1_c[b][:].bitcast(U16),
+                in_=w1_raw[:].bitcast(U16)[:, :, cols].rearrange("p a (m i) -> p a i m", i=PACK),
+            )
+            nc.vector.tensor_copy(
+                out=w1_s[b][:], in_=w1_sc_raw[:, :, cols].rearrange("p a (m i) -> p a i m", i=PACK)
+            )
+
+        v_w = {}
+        v_s = {}
+
+        def gather(h):
+            lst = pick[:, h * (BANK // 16) : (h + 1) * (BANK // 16)]
+            for a in range(PASSES):
+                v_s[a, h] = keep.tile([P, BANK], U8, name=f"v_s{a}{h}", align_bytes=64)
+                nc.vector.tensor_copy(out=v_s[a, h][:], in_=tab_sc[:, a, :].indirect(lst))
+            for a in range(PASSES):
+                v_w[a, h] = keep.tile([P, BANK], U32, name=f"v_w{a}{h}", align_bytes=64)
+                nc.vector.tensor_copy(out=v_w[a, h][:], in_=tab_w[a][:].bitcast(U32).indirect(lst))
+
+        d_t, r_t, m_t = {}, {}, {}
+
+        def residual(s, h):
+            b, i = divmod(s, PACK)
+            cols = slice(h * BANK, (h + 1) * BANK)
+            acc = psum.tile([P, BANK], F32, name="pred", tag="pred", bufs=2)
+            for a in range(PASSES):
+                nc.tensor.matmul_mx(
+                    out=acc[:],
+                    lhsT=w1_c[b][:, a, i, :].bitcast(FP4X4),
+                    lhsT_scale=w1_s[b][:, a, i, :],
+                    rhs=v_w[a, h][:].bitcast(FP8X4),
+                    rhs_scale=v_s[a, h][:],
+                    start=(a == 0),
+                    stop=(a == PASSES - 1),
+                )
+            if s not in d_t:
+                d_t[s] = ring.tile([P, S], F32, name="d_s", tag="d_s")
+            nc.vector.tensor_tensor(out=d_t[s][:, cols], in0=acc[:], in1=reads_t[s][:, cols], op=ALU.subtract)
+
+        def damp(s, cols):
+            b, i = divmod(s, PACK)
+            if s not in m_t:
+                r_t[s] = r_first[:] if s == 0 else z_plane(s - 1)
+                m_t[s] = ring.tile([P, S], F32, name="m_s", tag="m_s")
+            d, r, m = d_t[s][:, cols], r_t[s][:, cols], m_t[s][:, cols]
+            g = gain_t[:, b, i : i + 1]
+            if s in M1_ON_VECTOR:
+                nc.vector.scalar_tensor_tensor(
+                    out=m, in0=d, scalar=g, in1=wgs_t[:, cols], op0=ALU.mult, op1=ALU.mult
+                )
+            else:
+                nc.scalar.activation(out=m, in_=wgs_t[:, cols], func=ACT.Copy, scale=g)
+                nc.gpsimd.tensor_tensor(out=m, in0=m, in1=d, op=ALU.mult)
+            nc.scalar.activation(out=r, in_=d, func=ACT.Square)
+            nc.scalar.activation(out=r, in_=r, func=ACT.Abs_reciprocal_sqrt, bias=1.0)
+            nc.scalar.activation(out=r, in_=r, func=ACT.Square)
+            if not TT_SCATTER:
+                nc.gpsimd.tensor_tensor(out=m, in0=m, in1=r, op=ALU.mult)
+
+        def put(s, cols):
+            lst = place[:, cols.start // 16 : cols.stop // 16]
+            window = pages[s % 3][:].indirect(lst)
+            if TT_SCATTER:
+                nc.vector.tensor_tensor(out=window, in0=m_t[s][:, cols], in1=r_t[s][:, cols], op=ALU.mult)
+            else:
+                nc.vector.tensor_copy(out=window, in_=m_t[s][:, cols])
+
+        def update(s, cols, engine):
+            engine.tensor_tensor(
+                out=z_plane(s).bitcast(BF16)[:, cols], in0=cal_t[s][:, cols], in1=pages[s % 3][:, cols], op=ALU.subtract
+            )
+
+        woven = {}
+
+        def weave(key, rows, on_vector):
+            woven[key] = ring.tile([P, BANK, PACK], BF16, name="woven", tag="woven", align_bytes=64)
+            dst = woven[key][:].rearrange("p (c j) t -> p c t j", j=4)
+            src = rows.rearrange("p t (c j) -> p c t j", j=4)
+            if on_vector:
+                nc.vector.tensor_copy(out=dst, in_=src)
+            else:
+                nc.scalar.copy(out=dst, in_=src)
+
+        codes, scales = {}, {}
+
+        def quantise(key):
+            codes[key] = keep.tile([P, BANK], U32, name=f"codes_{key[0]}{key[1]}{key[2]}", align_bytes=64)
+            scales[key] = keep.tile([P, BANK], U8, name=f"scales_{key[0]}{key[1]}{key[2]}", align_bytes=64)
+            nc.vector.quantize_mx(
+                out=codes[key][:].bitcast(FP8X4),
+                scales=scales[key][:],
+                in_=woven[key][:].rearrange("p m t -> p (m t)"),
+            )
+
+        def z_chunk(b, c):
+            return z_rows[b][:].bitcast(BF16).rearrange("p (t m) -> p t m", t=PACK)[:, :, c * BANK : (c + 1) * BANK]
+
+        def prepare_w2(b):
+            raw = ring.tile([P, PACK, N], F32, name="w2_raw", tag="wide", align_bytes=64)
+            nc.sync.dma_start(out=raw[:], in_=w2[b * BANK : (b + 1) * BANK, :].rearrange("(p i) n -> p i n", i=PACK))
+            weave(("w", b, 0), raw[:], False)
+            quantise(("w", b, 0))
+
+        whole = slice(0, S)
+        halves = [slice(0, BANK), slice(BANK, S)]
+
+        order_w1(0)
+        order_w1(1)
+        gather(0)
+        residual(0, 0)
+        damp(0, halves[0])
+        gather(1)
+        load_reads(1)
+        residual(0, 1)
+        damp(0, halves[1])
+        put(0, halves[0])
+        for s in range(SLICES):
+            if s + 1 < SLICES:
+                if s + 2 < SLICES:
+                    load_reads(s + 2)
+                residual(s + 1, 0)
+                residual(s + 1, 1)
+                damp(s + 1, whole)
+            load_cal(s)
+            put(s, halves[1] if s == 0 else whole)
+            if s < PASSES:
+                prepare_w2(s)
+            if s >= 1:
+                engine = nc.vector if s - 1 in Z_ON_VECTOR else nc.gpsimd
+                for u in range(T2 // HALF):
+                    update(s - 1, slice(u * HALF, (u + 1) * HALF), engine)
+            if s >= PACK:
+                weave(("z", 0, s - PACK), z_chunk(0, s - PACK), False)
+                quantise(("z", 0, s - PACK))
+
+        last = SLICES - 1
+        chunks = T2 // BANK
+
+        def scores(c):
+            for n in range(N // P):
+                acc = psum.tile([P, BANK], F32, name="score", tag="score", bufs=6)
+                for b in range(PASSES):
+                    nc.tensor.matmul_mx(
+                        out=acc[:],
+                        lhsT=codes["w", b, 0][:, n * P : (n + 1) * P].bitcast(FP8X4),
+                        lhsT_scale=scales["w", b, 0][:, n * P : (n + 1) * P],
+                        rhs=codes["z", b, c][:].bitcast(FP8X4),
+                        rhs_scale=scales["z", b, c][:],
+                        start=(b == 0),
+                        stop=(b == PASSES - 1),
+                    )
+                res = ring.tile([P, BANK], F32, name="res", tag="res", bufs=6)
+                nc.scalar.copy(out=res[:], in_=acc[:])
+                nc.sync.dma_start(out=out[n * P : (n + 1) * P, c * BANK : (c + 1) * BANK], in_=res[:])
+
+        update(last, slice(0, BANK), nc.vector)
+        for c in range(chunks):
+            if c + 1 < chunks:
+                update(last, slice((c + 1) * BANK, (c + 2) * BANK), nc.vector)
+            weave(("z", 1, c), z_chunk(1, c), True)
+            if c >= 1:
+                quantise(("z", 1, c - 1))
+                scores(c - 1)
+        quantise(("z", 1, chunks - 1))
+        scores(chunks - 1)

@@ -1,6 +1,7 @@
 from contextlib import ExitStack
 
 import concourse.mybir as mybir
+from concourse.masks import make_identity
 
 K, T, S, T2, H, N = 1024, 2048, 1024, 2048, 1024, 512
 FLOPS = 2 * K * H * S + 2 * H * N * T2
@@ -21,11 +22,13 @@ PACK = 4
 PASSES = 2
 BANK = 512
 SLICES = PASSES * PACK
-HALF = 1024
-
-M1_ON_VECTOR = (3, 5, 7)
-TT_SCATTER = False
-Z_ON_VECTOR = ()
+CHUNKS = T2 // BANK
+PAGE_OF = (0, 1, 2, 3, 0, 1, 2, 2)
+CAL_SLOT = (2, 3, 0, 1, 4, 5, 6, 1)
+R_SLOT = ("r0", "r1", "r2", "r0", "r1", "wide2", "wide3", "wide0")
+PIECES = ((0, 0, 256), (0, 256, 512), (1, 0, 512), (2, 0, 512), (3, 0, 512))
+PRED_BANKS = (0, 1)
+ALL_BANKS = (2, 3, 4, 5, 6, 7, 0, 1)
 
 
 def tile_list_axle_calibration_audit_kernel(
@@ -36,64 +39,77 @@ def tile_list_axle_calibration_audit_kernel(
         keep = ctx.enter_context(tc.tile_pool(name="keep", bufs=1))
         ring = ctx.enter_context(tc.tile_pool(name="ring", bufs=3))
         psum = ctx.enter_context(tc.psum_pool(name="psum", bufs=1))
+        uses = {}
+
+        def next_bank(banks):
+            n = uses.get(banks, 0)
+            uses[banks] = n + 1
+            return psum.tile([P, BANK], F32, name="bank", tag=f"bank{banks[n % len(banks)]}")
 
         pick = keep.tile([P, S // 16], U16, name="pick")
         place = keep.tile([P, S // 16], U16, name="place")
 
-        tab_sc = ring.tile([P, PASSES, T], U8, name="tab_sc", tag="narrow", align_bytes=64)
-        w1_sc_raw = ring.tile([P, PASSES, H], U8, name="w1_sc_raw", tag="narrow", align_bytes=64)
-        nc.vector.memset(tab_sc[:].bitcast(I32), 0)
-        nc.vector.memset(w1_sc_raw[:].bitcast(I32), 0)
+        w1_sc_raw = keep.tile([P, PASSES, H], U8, name="w1_sc_raw", tag="rows1", align_bytes=64)
+        warm = keep.tile([P, 2], F32, name="warm")
+        v_s = keep.tile([P, PASSES, S], U8, name="v_s", align_bytes=64)
+        nc.gpsimd.memset(w1_sc_raw[:].bitcast(I32), 0)
+        nc.gpsimd.memset(warm[:, 0:1], 1.0)
+        nc.gpsimd.memset(v_s[:].bitcast(I32), 0)
         nc.sync.dma_start(pick[:], offs)
+        tab_sc = keep.tile([P, T], U8, name="tab_sc", tag="r0", align_bytes=64)
+        nc.sync.dma_start(
+            out=tab_sc[:].bitcast(I32),
+            in_=tab_scales.rearrange("a q n -> (a q) n").bitcast(I32).unsqueeze(0).broadcast_to([4, 32, T // 4]),
+        )
         nc.sync.dma_start(place[:], offs2)
         gain_t = keep.tile([P, PASSES, PACK], F32, name="gain_t")
         nc.sync.dma_start(out=gain_t[:], in_=gain.rearrange("(b p i) -> p b i", b=PASSES, i=PACK))
-        w1_raw = ring.tile([P, PASSES, 2 * H], U8, name="w1_raw", tag="wide", align_bytes=64)
+        w1_raw = keep.tile([P, PASSES, 2 * H], U8, name="w1_raw", tag="wgs", align_bytes=64)
         nc.sync.dma_start(out=w1_raw[:].bitcast(I32), in_=w1_words.rearrange("a p n -> p a n").bitcast(I32))
-        tab_w = [ring.tile([P, T], I32, name=f"tab_w{a}", tag="wide", align_bytes=64) for a in range(PASSES)]
+        tab_w = [keep.tile([P, T], I32, name=f"tab_w{a}", tag=f"late{a}", align_bytes=64) for a in range(PASSES)]
         for a in range(PASSES):
             nc.sync.dma_start(out=tab_w[a][:], in_=tab_words[a].rearrange("p t i -> p (t i)").bitcast(I32))
         for q in range(4):
             nc.scalar.dma_start(
-                out=tab_sc[32 * q : 32 * q + 4].bitcast(I32),
-                in_=tab_scales[:, 4 * q : 4 * q + 4, :].rearrange("a r n -> r a n").bitcast(I32),
-            )
-        for q in range(4):
-            nc.gpsimd.dma_start(
                 out=w1_sc_raw[32 * q : 32 * q + 4].bitcast(I32),
                 in_=w1_scales[:, 4 * q : 4 * q + 4, :].rearrange("a r n -> r a n").bitcast(I32),
             )
-        reads_v = reads.rearrange("(b p i) j -> b i p j", b=PASSES, i=PACK)
+        nc.scalar.activation(out=warm[:, 1:2], in_=warm[:, 0:1], func=ACT.Abs_reciprocal_sqrt, bias=1.0)
+        picked_sc = keep.tile([P, S], U8, name="picked_sc", tag="rows4", align_bytes=64)
+        nc.vector.tensor_copy(out=picked_sc[:], in_=tab_sc[:].indirect(pick[:]))
+        for a in range(PASSES):
+            for q in range(4):
+                row = 36 * q + 16 * a
+                nc.scalar.dma_start(
+                    out=v_s[32 * q : 32 * q + 4, a, :].bitcast(I32), in_=picked_sc[row : row + 4, :].bitcast(I32)
+                )
+        ident = keep.tile([P, P], F32, name="ident")
+        make_identity(nc, ident[:])
+
+        reads_v = reads.rearrange("(b p i) j -> b p (i j)", b=PASSES, i=PACK)
         cal_v = cal.rearrange("(b p i) m -> b i p m", b=PASSES, i=PACK)
-        reads_t = {}
+        d_t = {}
         cal_t = {}
 
-        def load_reads(s):
-            reads_t[s] = ring.tile([P, S], F32, name="reads_s", tag="narrow", align_bytes=64)
-            nc.sync.dma_start(out=reads_t[s][:], in_=reads_v[s // PACK, s % PACK])
+        def load_reads(first, count):
+            b, i = divmod(first, PACK)
+            rows = keep.tile([P, count * S], F32, name="rows", tag=f"rows{first}", align_bytes=64)
+            nc.sync.dma_start(out=rows[:], in_=reads_v[b][:, i * S : (i + count) * S])
+            for s in range(count):
+                d_t[first + s] = rows[:, s * S : (s + 1) * S]
 
         def load_cal(s):
-            cal_t[s] = ring.tile([P, T2], F32, name="cal_s", tag="wide", align_bytes=64)
+            cal_t[s] = keep.tile([P, T2], F32, name="cal_s", tag=f"wide{CAL_SLOT[s]}", align_bytes=64)
             nc.sync.dma_start(out=cal_t[s][:], in_=cal_v[s // PACK, s % PACK])
 
-        load_reads(0)
-        wgs_t = keep.tile([P, S], F32, name="wgs_t")
-        nc.sync.dma_start(out=wgs_t[:], in_=wgs)
+        load_reads(0, 1)
 
-        pages = [keep.tile([P, T2], F32, name=f"page{u}") for u in range(3)]
-        nc.vector.memset(pages[0][:], 0.0)
-        nc.gpsimd.memset(pages[1][:], 0.0)
-        nc.gpsimd.memset(pages[2][:], 0.0)
+        pages = [keep.tile([P, T2], F32, name=f"page{u}") for u in range(2)]
+        for page in pages:
+            nc.vector.memset(page[:], 0.0)
 
-        z_rows = [keep.tile([P, PACK * T2 // 2], F32, name=f"z_rows{b}", align_bytes=64) for b in range(PASSES)]
-        r_first = keep.tile([P, S], F32, name="r_first")
-
-        def z_plane(s):
-            b, i = divmod(s, PACK)
-            return z_rows[b][:, i * S : (i + 1) * S]
-
-        w1_c = [keep.tile([P, PASSES, PACK, 2 * P], U8, name=f"w1_c{b}", align_bytes=64) for b in range(PASSES)]
-        w1_s = [keep.tile([P, PASSES, PACK, P], U8, name=f"w1_s{b}", align_bytes=64) for b in range(PASSES)]
+        w1_c = [keep.tile([P, PASSES, PACK, 2 * P], U8, name=f"w1_c{b}", tag=("wide2", "wide6")[b], align_bytes=64) for b in range(PASSES)]
+        w1_s = [keep.tile([P, PASSES, PACK, P], U8, name=f"w1_s{b}", tag=("wide3", "w1_s")[b], align_bytes=64) for b in range(PASSES)]
 
         def order_w1(b):
             cols = slice(b * BANK, (b + 1) * BANK)
@@ -106,160 +122,259 @@ def tile_list_axle_calibration_audit_kernel(
             )
 
         v_w = {}
-        v_s = {}
 
         def gather(h):
             lst = pick[:, h * (BANK // 16) : (h + 1) * (BANK // 16)]
             for a in range(PASSES):
-                v_s[a, h] = keep.tile([P, BANK], U8, name=f"v_s{a}{h}", align_bytes=64)
-                nc.vector.tensor_copy(out=v_s[a, h][:], in_=tab_sc[:, a, :].indirect(lst))
-            for a in range(PASSES):
-                v_w[a, h] = keep.tile([P, BANK], U32, name=f"v_w{a}{h}", align_bytes=64)
+                v_w[a, h] = keep.tile([P, BANK], U32, name=f"v_w{a}{h}", tag=f"wide{(0, 1, 4, 5)[a + 2 * h]}", align_bytes=64)
                 nc.vector.tensor_copy(out=v_w[a, h][:], in_=tab_w[a][:].bitcast(U32).indirect(lst))
 
-        d_t, r_t, m_t = {}, {}, {}
+        r_t = {}
 
         def residual(s, h):
             b, i = divmod(s, PACK)
             cols = slice(h * BANK, (h + 1) * BANK)
-            acc = psum.tile([P, BANK], F32, name="pred", tag="pred", bufs=2)
+            acc = next_bank(PRED_BANKS)
             for a in range(PASSES):
                 nc.tensor.matmul_mx(
                     out=acc[:],
                     lhsT=w1_c[b][:, a, i, :].bitcast(FP4X4),
                     lhsT_scale=w1_s[b][:, a, i, :],
                     rhs=v_w[a, h][:].bitcast(FP8X4),
-                    rhs_scale=v_s[a, h][:],
+                    rhs_scale=v_s[:, a, cols],
                     start=(a == 0),
                     stop=(a == PASSES - 1),
                 )
-            if s not in d_t:
-                d_t[s] = ring.tile([P, S], F32, name="d_s", tag="d_s")
-            nc.vector.tensor_tensor(out=d_t[s][:, cols], in0=acc[:], in1=reads_t[s][:, cols], op=ALU.subtract)
+            nc.vector.tensor_tensor(out=d_t[s][:, cols], in0=d_t[s][:, cols], in1=acc[:], op=ALU.subtract)
 
         def damp(s, cols):
             b, i = divmod(s, PACK)
-            if s not in m_t:
-                r_t[s] = r_first[:] if s == 0 else z_plane(s - 1)
-                m_t[s] = ring.tile([P, S], F32, name="m_s", tag="m_s")
-            d, r, m = d_t[s][:, cols], r_t[s][:, cols], m_t[s][:, cols]
-            g = gain_t[:, b, i : i + 1]
-            if s in M1_ON_VECTOR:
-                nc.vector.scalar_tensor_tensor(
-                    out=m, in0=d, scalar=g, in1=wgs_t[:, cols], op0=ALU.mult, op1=ALU.mult
-                )
-            else:
-                nc.scalar.activation(out=m, in_=wgs_t[:, cols], func=ACT.Copy, scale=g)
-                nc.gpsimd.tensor_tensor(out=m, in0=m, in1=d, op=ALU.mult)
+            if s not in r_t:
+                r_t[s] = keep.tile([P, S], F32, name="r_s", tag=R_SLOT[s], align_bytes=64)
+            d, r = d_t[s][:, cols], r_t[s][:, cols]
             nc.scalar.activation(out=r, in_=d, func=ACT.Square)
             nc.scalar.activation(out=r, in_=r, func=ACT.Abs_reciprocal_sqrt, bias=1.0)
             nc.scalar.activation(out=r, in_=r, func=ACT.Square)
-            if not TT_SCATTER:
-                nc.gpsimd.tensor_tensor(out=m, in0=m, in1=r, op=ALU.mult)
+            nc.vector.scalar_tensor_tensor(
+                out=d, in0=d, scalar=gain_t[:, b, i : i + 1], in1=wgs_t[:, cols], op0=ALU.mult, op1=ALU.mult
+            )
 
         def put(s, cols):
-            lst = place[:, cols.start // 16 : cols.stop // 16]
-            window = pages[s % 3][:].indirect(lst)
-            if TT_SCATTER:
-                nc.vector.tensor_tensor(out=window, in0=m_t[s][:, cols], in1=r_t[s][:, cols], op=ALU.mult)
-            else:
-                nc.vector.tensor_copy(out=window, in_=m_t[s][:, cols])
+            window = pages[PAGE_OF[s]][:].indirect(place[:, cols.start // 16 : cols.stop // 16])
+            nc.vector.tensor_tensor(out=window, in0=d_t[s][:, cols], in1=r_t[s][:, cols], op=ALU.mult)
 
-        def update(s, cols, engine):
-            engine.tensor_tensor(
-                out=z_plane(s).bitcast(BF16)[:, cols], in0=cal_t[s][:, cols], in1=pages[s % 3][:, cols], op=ALU.subtract
+        turned = {}
+        steps = T2 // (2 * P)
+
+        def turn(pair, q):
+            acc = next_bank(ALL_BANKS)
+            for mb in range(2):
+                cols = slice((2 * q + mb) * P, (2 * q + mb + 1) * P)
+                for e in range(2):
+                    s = 2 * pair + e
+                    dst = acc[:, (2 * mb + e) * P : (2 * mb + e + 1) * P]
+                    nc.tensor.matmul(dst, cal_t[s][:, cols], ident[:], start=True, stop=False, is_transpose=True)
+                    nc.tensor.matmul(
+                        dst, pages[PAGE_OF[s]][:, cols], ident[:], start=False, stop=True, is_transpose=True
+                    )
+            if q == 0:
+                turned[pair] = keep.tile([P, steps * BANK], BF16, name="turned", tag=f"turned{pair}", align_bytes=64)
+            turned[pair, q] = turned[pair][:, q * BANK : (q + 1) * BANK]
+            nc.scalar.copy(
+                out=turned[pair, q].rearrange("m (b p e) -> m b p e", b=2, e=2),
+                in_=acc[:].rearrange("m (b e p) -> m b p e", b=2, e=2),
             )
 
         woven = {}
 
-        def weave(key, rows, on_vector):
-            woven[key] = ring.tile([P, BANK, PACK], BF16, name="woven", tag="woven", align_bytes=64)
-            dst = woven[key][:].rearrange("p (c j) t -> p c t j", j=4)
-            src = rows.rearrange("p t (c j) -> p c t j", j=4)
-            if on_vector:
-                nc.vector.tensor_copy(out=dst, in_=src)
+        def new_woven(key):
+            if key[:2] == ("z", 0):
+                woven[key] = keep.tile([P, BANK * PACK], BF16, name="woven0", tag=f"z_rows{key[2]}", align_bytes=64)
             else:
-                nc.scalar.copy(out=dst, in_=src)
+                woven[key] = ring.tile([P, BANK * PACK], BF16, name="woven", tag="woven", align_bytes=64)
+
+        def turn_back_woven(q):
+            key = ("z", 0, q // 2)
+            if key not in woven:
+                new_woven(key)
+            acc = next_bank(ALL_BANKS)
+            for u in range(2):
+                words = turned[u, q].bitcast(F32)
+                for mb in range(2):
+                    nc.tensor.transpose(
+                        acc[:, (2 * u + mb) * P : (2 * u + mb + 1) * P], words[:, mb * P : (mb + 1) * P], ident[:]
+                    )
+            dst = woven[key][:].bitcast(F32)[:, (q % 2) * BANK : (q % 2 + 1) * BANK]
+            nc.scalar.copy(out=dst.rearrange("p (m u) -> p m u", u=2), in_=acc[:].rearrange("p (u m) -> p m u", u=2))
+
+        pair_words = {}
+        z_rows = {}
+
+        def turn_back_words(c):
+            if c % 2 == 0:
+                both = keep.tile([P, 4 * BANK], F32, name="pair_words", tag=f"turned{c // 2}", align_bytes=64)
+                pair_words[c] = both[:, 0 : 2 * BANK]
+                pair_words[c + 1] = both[:, 2 * BANK : 4 * BANK]
+            acc = next_bank(ALL_BANKS)
+            for k in range(4):
+                words = turned[2, 2 * c + k // 2].bitcast(F32)
+                nc.tensor.transpose(acc[:, k * P : (k + 1) * P], words[:, (k % 2) * P : (k % 2 + 1) * P], ident[:])
+            nc.scalar.copy(out=pair_words[c][:, 0:BANK], in_=acc[:])
+
+        def update(s, c, lo, hi):
+            cols = slice(c * BANK + lo, c * BANK + hi)
+            e = s % 2
+            if c not in z_rows:
+                z_rows[c] = keep.tile([P, 2 * BANK], BF16, name="z_rows", tag=f"z_rows{c}", align_bytes=64)
+            nc.vector.tensor_tensor(
+                out=z_rows[c][:, e * BANK + lo : e * BANK + hi],
+                in0=cal_t[s][:, cols],
+                in1=pages[PAGE_OF[s]][:, cols],
+                op=ALU.add,
+            )
+
+        def pair_up(c, lo, hi):
+            move = nc.scalar.copy if c in (1, 2) else nc.vector.tensor_copy
+            move(
+                out=pair_words[c][:, BANK + lo : BANK + hi].bitcast(BF16).rearrange("p (k j e) -> p k e j", j=4, e=2),
+                in_=z_rows[c][:].rearrange("p (e m) -> p e m", e=2)[:, :, lo:hi].rearrange("p e (k j) -> p k e j", j=4),
+            )
+
+        def weave_words(c, lo, hi):
+            key = ("z", 1, c, lo)
+            new_woven(key)
+            nc.vector.tensor_copy(
+                out=woven[key][:, 0 : (hi - lo) * PACK].bitcast(F32).rearrange("p (k j u) -> p k u j", j=4, u=2),
+                in_=pair_words[c].rearrange("p (u m) -> p u m", u=2)[:, :, lo:hi].rearrange("p u (k j) -> p k u j", j=4),
+            )
+
+        def quantise_piece(c, lo, hi):
+            key = ("z", 1, c, lo)
+            codes[key] = keep.tile([P, hi - lo], U32, name=f"codes_z{c}_{lo}", align_bytes=64)[:]
+            scales[key] = keep.tile([P, hi - lo], U8, name=f"scales_z{c}_{lo}", align_bytes=64)
+            nc.vector.quantize_mx(
+                out=codes[key].bitcast(FP8X4), scales=scales[key][:], in_=woven[key][:, 0 : (hi - lo) * PACK]
+            )
 
         codes, scales = {}, {}
 
         def quantise(key):
-            codes[key] = keep.tile([P, BANK], U32, name=f"codes_{key[0]}{key[1]}{key[2]}", align_bytes=64)
+            if key not in codes:
+                codes[key] = keep.tile([P, BANK], U32, name=f"codes_{key[0]}{key[1]}{key[2]}", align_bytes=64)[:]
             scales[key] = keep.tile([P, BANK], U8, name=f"scales_{key[0]}{key[1]}{key[2]}", align_bytes=64)
-            nc.vector.quantize_mx(
-                out=codes[key][:].bitcast(FP8X4),
-                scales=scales[key][:],
-                in_=woven[key][:].rearrange("p m t -> p (m t)"),
-            )
-
-        def z_chunk(b, c):
-            return z_rows[b][:].bitcast(BF16).rearrange("p (t m) -> p t m", t=PACK)[:, :, c * BANK : (c + 1) * BANK]
+            nc.vector.quantize_mx(out=codes[key].bitcast(FP8X4), scales=scales[key][:], in_=woven[key][:])
 
         def prepare_w2(b):
-            raw = ring.tile([P, PACK, N], F32, name="w2_raw", tag="wide", align_bytes=64)
+            raw = keep.tile([P, PACK, N], F32, name="w2_raw", tag=f"wide{b}", align_bytes=64)
             nc.sync.dma_start(out=raw[:], in_=w2[b * BANK : (b + 1) * BANK, :].rearrange("(p i) n -> p i n", i=PACK))
-            weave(("w", b, 0), raw[:], False)
-            quantise(("w", b, 0))
+            key = ("w", b, 0)
+            new_woven(key)
+            nc.scalar.copy(
+                out=woven[key][:].rearrange("p (k j t) -> p k t j", j=4, t=PACK),
+                in_=raw[:].rearrange("p t (k j) -> p k t j", j=4),
+            )
 
         whole = slice(0, S)
         halves = [slice(0, BANK), slice(BANK, S)]
 
         order_w1(0)
         order_w1(1)
+        wgs_t = keep.tile([P, S], F32, name="wgs_t", tag="wgs", align_bytes=64)
+        nc.scalar.dma_start(out=wgs_t[:], in_=wgs)
+        load_reads(1, PACK - 1)
+        load_reads(PACK, PACK)
         gather(0)
         residual(0, 0)
         damp(0, halves[0])
         gather(1)
-        load_reads(1)
         residual(0, 1)
         damp(0, halves[1])
+        for s in range(1, SLICES):
+            residual(s, 0)
+            residual(s, 1)
+            if s < 3:
+                damp(s, whole)
+            if s == 3:
+                load_cal(0)
+                load_cal(1)
+        prepare_w2(0)
+        prepare_w2(1)
+        for s in (2, 3, 4, 5, 6):
+            load_cal(s)
+        for a in range(PASSES):
+            page = keep.tile([P, T2], F32, name=f"page{2 + a}", tag=f"late{a}", align_bytes=64)
+            nc.vector.memset(page[:], 0.0)
+            pages.append(page)
         put(0, halves[0])
         for s in range(SLICES):
-            if s + 1 < SLICES:
-                if s + 2 < SLICES:
-                    load_reads(s + 2)
-                residual(s + 1, 0)
-                residual(s + 1, 1)
-                damp(s + 1, whole)
-            load_cal(s)
             put(s, halves[1] if s == 0 else whole)
-            if s < PASSES:
-                prepare_w2(s)
-            if s >= 1:
-                engine = nc.vector if s - 1 in Z_ON_VECTOR else nc.gpsimd
-                for u in range(T2 // HALF):
-                    update(s - 1, slice(u * HALF, (u + 1) * HALF), engine)
-            if s >= PACK:
-                weave(("z", 0, s - PACK), z_chunk(0, s - PACK), False)
-                quantise(("z", 0, s - PACK))
-
+            if s < 2:
+                damp(s + 3, whole)
+            if s == 1:
+                for q in range(steps):
+                    turn(0, q)
+                damp(5, whole)
+                damp(6, whole)
+            if s == 3:
+                for q in range(steps):
+                    turn(1, q)
+                damp(7, whole)
+                load_cal(7)
+                for q in range(steps):
+                    turn_back_woven(q)
+            if s == 4:
+                w2_codes = keep.tile([P, PASSES * N], U32, name="w2_codes", tag="r1", align_bytes=64)
+                for b in range(PASSES):
+                    codes["w", b, 0] = w2_codes[:, b * N : (b + 1) * N]
+                    quantise(("w", b, 0))
+            if s == 5:
+                for q in range(steps):
+                    turn(2, q)
+                    if q >= 2 and q % 2 == 0:
+                        turn_back_words(q // 2 - 1)
+                turn_back_words(CHUNKS - 1)
+            if s == 6:
+                z_codes = keep.tile([P, T2], U32, name="z_codes", tag="wide3", align_bytes=64)
+                for c in range(CHUNKS):
+                    codes["z", 0, c] = z_codes[:, c * BANK : (c + 1) * BANK]
+                    quantise(("z", 0, c))
+                for c in range(CHUNKS):
+                    update(s, c, 0, BANK)
         last = SLICES - 1
-        chunks = T2 // BANK
 
-        def scores(c):
+        def scores(index, c, lo, hi):
             for n in range(N // P):
-                acc = psum.tile([P, BANK], F32, name="score", tag="score", bufs=6)
+                acc = next_bank(ALL_BANKS)
+                moving = (
+                    (codes["z", 0, c][:, lo:hi], scales["z", 0, c][:, lo:hi]),
+                    (codes["z", 1, c, lo], scales["z", 1, c, lo][:]),
+                )
                 for b in range(PASSES):
                     nc.tensor.matmul_mx(
-                        out=acc[:],
+                        out=acc[:, 0 : hi - lo],
                         lhsT=codes["w", b, 0][:, n * P : (n + 1) * P].bitcast(FP8X4),
                         lhsT_scale=scales["w", b, 0][:, n * P : (n + 1) * P],
-                        rhs=codes["z", b, c][:].bitcast(FP8X4),
-                        rhs_scale=scales["z", b, c][:],
+                        rhs=moving[b][0].bitcast(FP8X4),
+                        rhs_scale=moving[b][1],
                         start=(b == 0),
                         stop=(b == PASSES - 1),
                     )
-                res = ring.tile([P, BANK], F32, name="res", tag="res", bufs=6)
-                nc.scalar.copy(out=res[:], in_=acc[:])
-                nc.sync.dma_start(out=out[n * P : (n + 1) * P, c * BANK : (c + 1) * BANK], in_=res[:])
+                res = ring.tile([P, BANK], F32, name="res", tag="res", bufs=8)
+                if index >= len(PIECES) - 2 and n % 2 == 1:
+                    nc.vector.tensor_copy(out=res[:, 0 : hi - lo], in_=acc[:, 0 : hi - lo])
+                else:
+                    nc.scalar.copy(out=res[:, 0 : hi - lo], in_=acc[:, 0 : hi - lo])
+                nc.sync.dma_start(
+                    out=out[n * P : (n + 1) * P, c * BANK + lo : c * BANK + hi], in_=res[:, 0 : hi - lo]
+                )
 
-        update(last, slice(0, BANK), nc.vector)
-        for c in range(chunks):
-            if c + 1 < chunks:
-                update(last, slice((c + 1) * BANK, (c + 2) * BANK), nc.vector)
-            weave(("z", 1, c), z_chunk(1, c), True)
-            if c >= 1:
-                quantise(("z", 1, c - 1))
-                scores(c - 1)
-        quantise(("z", 1, chunks - 1))
-        scores(chunks - 1)
+        for step in range(len(PIECES) + 3):
+            if 0 <= step - 3 < len(PIECES):
+                quantise_piece(*PIECES[step - 3])
+                scores(step - 3, *PIECES[step - 3])
+            if 0 <= step - 2 < len(PIECES):
+                weave_words(*PIECES[step - 2])
+            if 0 <= step - 1 < len(PIECES):
+                pair_up(*PIECES[step - 1])
+            if step < len(PIECES):
+                update(last, *PIECES[step])

@@ -26,7 +26,7 @@ CHUNKS = T2 // BANK
 PAGE_OF = (0, 1, 2, 3, 0, 1, 2, 2)
 CAL_SLOT = (2, 3, 0, 1, 4, 5, 6, 1)
 R_SLOT = ("r0", "r1", "r2", "r0", "r1", "wide2", "wide3", "wide0")
-PIECES = ((0, 0, 256), (0, 256, 512), (1, 0, 512), (2, 0, 512), (3, 0, 512))
+PIECES = ((0, 0, 128), (0, 128, 256), (0, 256, 512), (1, 0, 512), (2, 0, 512), (3, 0, 256), (3, 256, 512))
 PRED_BANKS = (0, 1)
 ALL_BANKS = (2, 3, 4, 5, 6, 7, 0, 1)
 
@@ -234,8 +234,7 @@ def tile_list_axle_calibration_audit_kernel(
             )
 
         def pair_up(c, lo, hi):
-            move = nc.scalar.copy if c in (1, 2) else nc.vector.tensor_copy
-            move(
+            nc.vector.tensor_copy(
                 out=pair_words[c][:, BANK + lo : BANK + hi].bitcast(BF16).rearrange("p (k j e) -> p k e j", j=4, e=2),
                 in_=z_rows[c][:].rearrange("p (e m) -> p e m", e=2)[:, :, lo:hi].rearrange("p e (k j) -> p k e j", j=4),
             )
@@ -342,6 +341,10 @@ def tile_list_axle_calibration_audit_kernel(
                     update(s, c, 0, BANK)
         last = SLICES - 1
 
+        staged = [
+            keep.tile([P, T2], F32, name="staged", tag=tag, align_bytes=64) for tag in ("wide4", "wide5", "wide2", "rows1")
+        ]
+
         def scores(index, c, lo, hi):
             for n in range(N // P):
                 acc = next_bank(ALL_BANKS)
@@ -359,22 +362,18 @@ def tile_list_axle_calibration_audit_kernel(
                         start=(b == 0),
                         stop=(b == PASSES - 1),
                     )
-                res = ring.tile([P, BANK], F32, name="res", tag="res", bufs=8)
-                if index >= len(PIECES) - 2 and n % 2 == 1:
-                    nc.vector.tensor_copy(out=res[:, 0 : hi - lo], in_=acc[:, 0 : hi - lo])
+                res = staged[n][:, c * BANK + lo : c * BANK + hi]
+                if index == len(PIECES) - 2:
+                    nc.vector.tensor_copy(out=res, in_=acc[:, 0 : hi - lo])
                 else:
-                    nc.scalar.copy(out=res[:, 0 : hi - lo], in_=acc[:, 0 : hi - lo])
+                    nc.scalar.copy(out=res, in_=acc[:, 0 : hi - lo])
                 nc.sync.dma_start(
-                    out=out[n * P : (n + 1) * P, c * BANK + lo : c * BANK + hi], in_=res[:, 0 : hi - lo]
+                    out=out[n * P : (n + 1) * P, c * BANK + lo : c * BANK + hi], in_=res
                 )
 
-        for step in range(len(PIECES) + 3):
-            if 0 <= step - 3 < len(PIECES):
-                quantise_piece(*PIECES[step - 3])
-                scores(step - 3, *PIECES[step - 3])
-            if 0 <= step - 2 < len(PIECES):
-                weave_words(*PIECES[step - 2])
-            if 0 <= step - 1 < len(PIECES):
-                pair_up(*PIECES[step - 1])
-            if step < len(PIECES):
-                update(last, *PIECES[step])
+        for index, piece in enumerate(PIECES):
+            update(last, *piece)
+            pair_up(*piece)
+            weave_words(*piece)
+            quantise_piece(*piece)
+            scores(index, *piece)

@@ -21,12 +21,18 @@ P = 128
 PACK = 4
 PASSES = 2
 BANK = 512
+QUADS = 4
+RUN = 4
 SLICES = PASSES * PACK
 CHUNKS = T2 // BANK
+STEPS = T2 // (2 * P)
+
 PAGE_OF = (0, 1, 2, 3, 0, 1, 2, 2)
-CAL_SLOT = (2, 3, 0, 1, 4, 5, 6, 1)
-R_SLOT = ("r0", "r1", "r2", "r0", "r1", "wide2", "wide3", "wide0")
-PIECES = ((0, 0, 128), (0, 128, 256), (0, 256, 512), (1, 0, 512), (2, 0, 512), (3, 0, 256), (3, 256, 512))
+CAL_SLOT = ("wide2", "wide3", "wide0", "wide1", "wide4", "wide5", "wide6", "wide1")
+DAMP_SLOT = ("damp0", "damp1", "damp2", "damp0", "damp1", "wide2", "wide3", "wide0")
+PICKED_SLOT = ("wide0", "wide1", "wide4", "wide5")
+STAGE_SLOT = ("wide4", "wide5", "wide2", "rows1")
+PIECES = ((0, 0, 256), (0, 256, 512), (1, 0, 512), (2, 0, 512), (3, 0, 512))
 PRED_BANKS = (0, 1)
 ALL_BANKS = (2, 3, 4, 5, 6, 7, 0, 1)
 
@@ -56,10 +62,10 @@ def tile_list_axle_calibration_audit_kernel(
         nc.gpsimd.memset(warm[:, 0:1], 1.0)
         nc.gpsimd.memset(v_s[:].bitcast(I32), 0)
         nc.sync.dma_start(pick[:], offs)
-        tab_sc = keep.tile([P, T], U8, name="tab_sc", tag="r0", align_bytes=64)
+        tab_sc = keep.tile([P, T], U8, name="tab_sc", tag="damp0", align_bytes=64)
         nc.sync.dma_start(
             out=tab_sc[:].bitcast(I32),
-            in_=tab_scales.rearrange("a q n -> (a q) n").bitcast(I32).unsqueeze(0).broadcast_to([4, 32, T // 4]),
+            in_=tab_scales.rearrange("a q n -> (a q) n").bitcast(I32).unsqueeze(0).broadcast_to([QUADS, 32, T // 4]),
         )
         nc.sync.dma_start(place[:], offs2)
         gain_t = keep.tile([P, PASSES, PACK], F32, name="gain_t")
@@ -69,7 +75,7 @@ def tile_list_axle_calibration_audit_kernel(
         tab_w = [keep.tile([P, T], I32, name=f"tab_w{a}", tag=f"late{a}", align_bytes=64) for a in range(PASSES)]
         for a in range(PASSES):
             nc.sync.dma_start(out=tab_w[a][:], in_=tab_words[a].rearrange("p t i -> p (t i)").bitcast(I32))
-        for q in range(4):
+        for q in range(QUADS):
             nc.scalar.dma_start(
                 out=w1_sc_raw[32 * q : 32 * q + 4].bitcast(I32),
                 in_=w1_scales[:, 4 * q : 4 * q + 4, :].rearrange("a r n -> r a n").bitcast(I32),
@@ -78,8 +84,8 @@ def tile_list_axle_calibration_audit_kernel(
         picked_sc = keep.tile([P, S], U8, name="picked_sc", tag="rows4", align_bytes=64)
         nc.vector.tensor_copy(out=picked_sc[:], in_=tab_sc[:].indirect(pick[:]))
         for a in range(PASSES):
-            for q in range(4):
-                row = 36 * q + 16 * a
+            for q in range(QUADS):
+                row = 32 * q + 16 * a + 4 * q
                 nc.scalar.dma_start(
                     out=v_s[32 * q : 32 * q + 4, a, :].bitcast(I32), in_=picked_sc[row : row + 4, :].bitcast(I32)
                 )
@@ -88,7 +94,7 @@ def tile_list_axle_calibration_audit_kernel(
 
         reads_v = reads.rearrange("(b p i) j -> b p (i j)", b=PASSES, i=PACK)
         cal_v = cal.rearrange("(b p i) m -> b i p m", b=PASSES, i=PACK)
-        d_t = {}
+        resid = {}
         cal_t = {}
 
         def load_reads(first, count):
@@ -96,10 +102,10 @@ def tile_list_axle_calibration_audit_kernel(
             rows = keep.tile([P, count * S], F32, name="rows", tag=f"rows{first}", align_bytes=64)
             nc.sync.dma_start(out=rows[:], in_=reads_v[b][:, i * S : (i + count) * S])
             for s in range(count):
-                d_t[first + s] = rows[:, s * S : (s + 1) * S]
+                resid[first + s] = rows[:, s * S : (s + 1) * S]
 
         def load_cal(s):
-            cal_t[s] = keep.tile([P, T2], F32, name="cal_s", tag=f"wide{CAL_SLOT[s]}", align_bytes=64)
+            cal_t[s] = keep.tile([P, T2], F32, name="cal_s", tag=CAL_SLOT[s], align_bytes=64)
             nc.sync.dma_start(out=cal_t[s][:], in_=cal_v[s // PACK, s % PACK])
 
         load_reads(0, 1)
@@ -108,8 +114,14 @@ def tile_list_axle_calibration_audit_kernel(
         for page in pages:
             nc.vector.memset(page[:], 0.0)
 
-        w1_c = [keep.tile([P, PASSES, PACK, 2 * P], U8, name=f"w1_c{b}", tag=("wide2", "wide6")[b], align_bytes=64) for b in range(PASSES)]
-        w1_s = [keep.tile([P, PASSES, PACK, P], U8, name=f"w1_s{b}", tag=("wide3", "w1_s")[b], align_bytes=64) for b in range(PASSES)]
+        w1_c = [
+            keep.tile([P, PASSES, PACK, 2 * P], U8, name=f"w1_c{b}", tag=("wide2", "wide6")[b], align_bytes=64)
+            for b in range(PASSES)
+        ]
+        w1_s = [
+            keep.tile([P, PASSES, PACK, P], U8, name=f"w1_s{b}", tag=("wide3", "w1_s")[b], align_bytes=64)
+            for b in range(PASSES)
+        ]
 
         def order_w1(b):
             cols = slice(b * BANK, (b + 1) * BANK)
@@ -124,12 +136,10 @@ def tile_list_axle_calibration_audit_kernel(
         v_w = {}
 
         def gather(h):
-            lst = pick[:, h * (BANK // 16) : (h + 1) * (BANK // 16)]
+            entries = pick[:, h * (BANK // 16) : (h + 1) * (BANK // 16)]
             for a in range(PASSES):
-                v_w[a, h] = keep.tile([P, BANK], U32, name=f"v_w{a}{h}", tag=f"wide{(0, 1, 4, 5)[a + 2 * h]}", align_bytes=64)
-                nc.vector.tensor_copy(out=v_w[a, h][:], in_=tab_w[a][:].bitcast(U32).indirect(lst))
-
-        r_t = {}
+                v_w[a, h] = keep.tile([P, BANK], U32, name=f"v_w{a}{h}", tag=PICKED_SLOT[a + 2 * h], align_bytes=64)
+                nc.vector.tensor_copy(out=v_w[a, h][:], in_=tab_w[a][:].bitcast(U32).indirect(entries))
 
         def residual(s, h):
             b, i = divmod(s, PACK)
@@ -145,28 +155,29 @@ def tile_list_axle_calibration_audit_kernel(
                     start=(a == 0),
                     stop=(a == PASSES - 1),
                 )
-            nc.vector.tensor_tensor(out=d_t[s][:, cols], in0=d_t[s][:, cols], in1=acc[:], op=ALU.subtract)
+            nc.vector.tensor_tensor(out=resid[s][:, cols], in0=resid[s][:, cols], in1=acc[:], op=ALU.subtract)
+
+        damping = {}
 
         def damp(s, cols):
             b, i = divmod(s, PACK)
-            if s not in r_t:
-                r_t[s] = keep.tile([P, S], F32, name="r_s", tag=R_SLOT[s], align_bytes=64)
-            d, r = d_t[s][:, cols], r_t[s][:, cols]
-            nc.scalar.activation(out=r, in_=d, func=ACT.Square)
-            nc.scalar.activation(out=r, in_=r, func=ACT.Abs_reciprocal_sqrt, bias=1.0)
-            nc.scalar.activation(out=r, in_=r, func=ACT.Square)
+            if s not in damping:
+                damping[s] = keep.tile([P, S], F32, name="damping", tag=DAMP_SLOT[s], align_bytes=64)
+            d, f = resid[s][:, cols], damping[s][:, cols]
+            nc.scalar.activation(out=f, in_=d, func=ACT.Square)
+            nc.scalar.activation(out=f, in_=f, func=ACT.Abs_reciprocal_sqrt, bias=1.0)
+            nc.scalar.activation(out=f, in_=f, func=ACT.Square)
             nc.vector.scalar_tensor_tensor(
                 out=d, in0=d, scalar=gain_t[:, b, i : i + 1], in1=wgs_t[:, cols], op0=ALU.mult, op1=ALU.mult
             )
 
         def put(s, cols):
             window = pages[PAGE_OF[s]][:].indirect(place[:, cols.start // 16 : cols.stop // 16])
-            nc.vector.tensor_tensor(out=window, in0=d_t[s][:, cols], in1=r_t[s][:, cols], op=ALU.mult)
+            nc.vector.tensor_tensor(out=window, in0=resid[s][:, cols], in1=damping[s][:, cols], op=ALU.mult)
 
         turned = {}
-        steps = T2 // (2 * P)
 
-        def turn(pair, q):
+        def turn_step(pair, q):
             acc = next_bank(ALL_BANKS)
             for mb in range(2):
                 cols = slice((2 * q + mb) * P, (2 * q + mb + 1) * P)
@@ -178,12 +189,16 @@ def tile_list_axle_calibration_audit_kernel(
                         dst, pages[PAGE_OF[s]][:, cols], ident[:], start=False, stop=True, is_transpose=True
                     )
             if q == 0:
-                turned[pair] = keep.tile([P, steps * BANK], BF16, name="turned", tag=f"turned{pair}", align_bytes=64)
+                turned[pair] = keep.tile([P, STEPS * BANK], BF16, name="turned", tag=f"turned{pair}", align_bytes=64)
             turned[pair, q] = turned[pair][:, q * BANK : (q + 1) * BANK]
             nc.scalar.copy(
                 out=turned[pair, q].rearrange("m (b p e) -> m b p e", b=2, e=2),
                 in_=acc[:].rearrange("m (b e p) -> m b p e", b=2, e=2),
             )
+
+        def turn(pair):
+            for q in range(STEPS):
+                turn_step(pair, q)
 
         woven = {}
 
@@ -216,9 +231,11 @@ def tile_list_axle_calibration_audit_kernel(
                 pair_words[c] = both[:, 0 : 2 * BANK]
                 pair_words[c + 1] = both[:, 2 * BANK : 4 * BANK]
             acc = next_bank(ALL_BANKS)
-            for k in range(4):
-                words = turned[2, 2 * c + k // 2].bitcast(F32)
-                nc.tensor.transpose(acc[:, k * P : (k + 1) * P], words[:, (k % 2) * P : (k % 2 + 1) * P], ident[:])
+            for blk in range(BANK // P):
+                words = turned[2, 2 * c + blk // 2].bitcast(F32)
+                nc.tensor.transpose(
+                    acc[:, blk * P : (blk + 1) * P], words[:, (blk % 2) * P : (blk % 2 + 1) * P], ident[:]
+                )
             nc.scalar.copy(out=pair_words[c][:, 0:BANK], in_=acc[:])
 
         def update(s, c, lo, hi):
@@ -234,43 +251,36 @@ def tile_list_axle_calibration_audit_kernel(
             )
 
         def pair_up(c, lo, hi):
+            rows = z_rows[c][:].rearrange("p (e m) -> p e m", e=2)[:, :, lo:hi]
             nc.vector.tensor_copy(
-                out=pair_words[c][:, BANK + lo : BANK + hi].bitcast(BF16).rearrange("p (k j e) -> p k e j", j=4, e=2),
-                in_=z_rows[c][:].rearrange("p (e m) -> p e m", e=2)[:, :, lo:hi].rearrange("p e (k j) -> p k e j", j=4),
+                out=pair_words[c][:, BANK + lo : BANK + hi].bitcast(BF16).rearrange("p (k j e) -> p k e j", j=RUN, e=2),
+                in_=rows.rearrange("p e (k j) -> p k e j", j=RUN),
             )
 
         def weave_words(c, lo, hi):
             key = ("z", 1, c, lo)
             new_woven(key)
+            rows = pair_words[c].rearrange("p (u m) -> p u m", u=2)[:, :, lo:hi]
             nc.vector.tensor_copy(
-                out=woven[key][:, 0 : (hi - lo) * PACK].bitcast(F32).rearrange("p (k j u) -> p k u j", j=4, u=2),
-                in_=pair_words[c].rearrange("p (u m) -> p u m", u=2)[:, :, lo:hi].rearrange("p u (k j) -> p k u j", j=4),
-            )
-
-        def quantise_piece(c, lo, hi):
-            key = ("z", 1, c, lo)
-            codes[key] = keep.tile([P, hi - lo], U32, name=f"codes_z{c}_{lo}", align_bytes=64)[:]
-            scales[key] = keep.tile([P, hi - lo], U8, name=f"scales_z{c}_{lo}", align_bytes=64)
-            nc.vector.quantize_mx(
-                out=codes[key].bitcast(FP8X4), scales=scales[key][:], in_=woven[key][:, 0 : (hi - lo) * PACK]
+                out=woven[key][:, 0 : (hi - lo) * PACK].bitcast(F32).rearrange("p (k j u) -> p k u j", j=RUN, u=2),
+                in_=rows.rearrange("p u (k j) -> p k u j", j=RUN),
             )
 
         codes, scales = {}, {}
 
-        def quantise(key):
-            if key not in codes:
-                codes[key] = keep.tile([P, BANK], U32, name=f"codes_{key[0]}{key[1]}{key[2]}", align_bytes=64)[:]
-            scales[key] = keep.tile([P, BANK], U8, name=f"scales_{key[0]}{key[1]}{key[2]}", align_bytes=64)
-            nc.vector.quantize_mx(out=codes[key].bitcast(FP8X4), scales=scales[key][:], in_=woven[key][:])
+        def quantise(key, dst, width):
+            codes[key] = dst
+            scales[key] = keep.tile([P, width], U8, name="scales_" + "_".join(map(str, key)), align_bytes=64)
+            nc.vector.quantize_mx(out=dst.bitcast(FP8X4), scales=scales[key][:], in_=woven[key][:, 0 : width * PACK])
 
-        def prepare_w2(b):
+        def weave_w2(b):
             raw = keep.tile([P, PACK, N], F32, name="w2_raw", tag=f"wide{b}", align_bytes=64)
             nc.sync.dma_start(out=raw[:], in_=w2[b * BANK : (b + 1) * BANK, :].rearrange("(p i) n -> p i n", i=PACK))
-            key = ("w", b, 0)
+            key = ("w", b)
             new_woven(key)
             nc.scalar.copy(
-                out=woven[key][:].rearrange("p (k j t) -> p k t j", j=4, t=PACK),
-                in_=raw[:].rearrange("p t (k j) -> p k t j", j=4),
+                out=woven[key][:].rearrange("p (k j t) -> p k t j", j=RUN, t=PACK),
+                in_=raw[:].rearrange("p t (k j) -> p k t j", j=RUN),
             )
 
         whole = slice(0, S)
@@ -282,98 +292,97 @@ def tile_list_axle_calibration_audit_kernel(
         nc.scalar.dma_start(out=wgs_t[:], in_=wgs)
         load_reads(1, PACK - 1)
         load_reads(PACK, PACK)
-        gather(0)
-        residual(0, 0)
-        damp(0, halves[0])
-        gather(1)
-        residual(0, 1)
-        damp(0, halves[1])
+        for h in range(2):
+            gather(h)
+            residual(0, h)
+            damp(0, halves[h])
         for s in range(1, SLICES):
             residual(s, 0)
             residual(s, 1)
             if s < 3:
                 damp(s, whole)
-            if s == 3:
+            if s == PACK - 1:
                 load_cal(0)
                 load_cal(1)
-        prepare_w2(0)
-        prepare_w2(1)
-        for s in (2, 3, 4, 5, 6):
+        weave_w2(0)
+        weave_w2(1)
+        for s in range(2, SLICES - 1):
             load_cal(s)
         for a in range(PASSES):
             page = keep.tile([P, T2], F32, name=f"page{2 + a}", tag=f"late{a}", align_bytes=64)
             nc.vector.memset(page[:], 0.0)
             pages.append(page)
+
         put(0, halves[0])
-        for s in range(SLICES):
-            put(s, halves[1] if s == 0 else whole)
-            if s < 2:
-                damp(s + 3, whole)
-            if s == 1:
-                for q in range(steps):
-                    turn(0, q)
-                damp(5, whole)
-                damp(6, whole)
-            if s == 3:
-                for q in range(steps):
-                    turn(1, q)
-                damp(7, whole)
-                load_cal(7)
-                for q in range(steps):
-                    turn_back_woven(q)
-            if s == 4:
-                w2_codes = keep.tile([P, PASSES * N], U32, name="w2_codes", tag="r1", align_bytes=64)
-                for b in range(PASSES):
-                    codes["w", b, 0] = w2_codes[:, b * N : (b + 1) * N]
-                    quantise(("w", b, 0))
-            if s == 5:
-                for q in range(steps):
-                    turn(2, q)
-                    if q >= 2 and q % 2 == 0:
-                        turn_back_words(q // 2 - 1)
-                turn_back_words(CHUNKS - 1)
-            if s == 6:
-                z_codes = keep.tile([P, T2], U32, name="z_codes", tag="wide3", align_bytes=64)
-                for c in range(CHUNKS):
-                    codes["z", 0, c] = z_codes[:, c * BANK : (c + 1) * BANK]
-                    quantise(("z", 0, c))
-                for c in range(CHUNKS):
-                    update(s, c, 0, BANK)
-        last = SLICES - 1
+        put(0, halves[1])
+        damp(3, whole)
+        put(1, whole)
+        damp(4, whole)
+        turn(0)
+        damp(5, whole)
+        damp(6, whole)
+        put(2, whole)
+        put(3, whole)
+        turn(1)
+        damp(7, whole)
+        load_cal(7)
+        for q in range(STEPS):
+            turn_back_woven(q)
+        put(4, whole)
+        w2_codes = keep.tile([P, PASSES * N], U32, name="w2_codes", tag=DAMP_SLOT[4], align_bytes=64)
+        for b in range(PASSES):
+            quantise(("w", b), w2_codes[:, b * N : (b + 1) * N], N)
+        put(5, whole)
+        for q in range(STEPS):
+            turn_step(2, q)
+            if q >= 2 and q % 2 == 0:
+                turn_back_words(q // 2 - 1)
+        turn_back_words(CHUNKS - 1)
+        put(6, whole)
+        z_codes = keep.tile([P, T2], U32, name="z_codes", tag=DAMP_SLOT[6], align_bytes=64)
+        for c in range(CHUNKS):
+            quantise(("z", 0, c), z_codes[:, c * BANK : (c + 1) * BANK], BANK)
+        for c in range(CHUNKS):
+            update(6, c, 0, BANK)
+        put(7, whole)
 
-        staged = [
-            keep.tile([P, T2], F32, name="staged", tag=tag, align_bytes=64) for tag in ("wide4", "wide5", "wide2", "rows1")
-        ]
+        staged = [keep.tile([P, T2], F32, name="staged", tag=tag, align_bytes=64) for tag in STAGE_SLOT]
+        out_v = out.rearrange("(n p) m -> p n m", p=P)
 
-        def scores(index, c, lo, hi):
+        def scores(c, lo, hi, shared):
+            width = hi - lo
+            rows = staged[c][:, (N // P) * lo : (N // P) * hi]
+            moving = (
+                (codes["z", 0, c][:, lo:hi], scales["z", 0, c][:, lo:hi]),
+                (codes["z", 1, c, lo], scales["z", 1, c, lo][:]),
+            )
             for n in range(N // P):
                 acc = next_bank(ALL_BANKS)
-                moving = (
-                    (codes["z", 0, c][:, lo:hi], scales["z", 0, c][:, lo:hi]),
-                    (codes["z", 1, c, lo], scales["z", 1, c, lo][:]),
-                )
                 for b in range(PASSES):
                     nc.tensor.matmul_mx(
-                        out=acc[:, 0 : hi - lo],
-                        lhsT=codes["w", b, 0][:, n * P : (n + 1) * P].bitcast(FP8X4),
-                        lhsT_scale=scales["w", b, 0][:, n * P : (n + 1) * P],
+                        out=acc[:, 0:width],
+                        lhsT=codes["w", b][:, n * P : (n + 1) * P].bitcast(FP8X4),
+                        lhsT_scale=scales["w", b][:, n * P : (n + 1) * P],
                         rhs=moving[b][0].bitcast(FP8X4),
                         rhs_scale=moving[b][1],
                         start=(b == 0),
                         stop=(b == PASSES - 1),
                     )
-                res = staged[n][:, c * BANK + lo : c * BANK + hi]
-                if index == len(PIECES) - 2:
-                    nc.vector.tensor_copy(out=res, in_=acc[:, 0 : hi - lo])
+                res = rows[:, n * width : (n + 1) * width]
+                if shared and n % 2 == 1:
+                    nc.vector.tensor_copy(out=res, in_=acc[:, 0:width])
                 else:
-                    nc.scalar.copy(out=res, in_=acc[:, 0 : hi - lo])
-                nc.sync.dma_start(
-                    out=out[n * P : (n + 1) * P, c * BANK + lo : c * BANK + hi], in_=res
-                )
+                    nc.scalar.copy(out=res, in_=acc[:, 0:width])
+                if n % 2 == 1:
+                    nc.sync.dma_start(
+                        out=out_v[:, n - 1 : n + 1, c * BANK + lo : c * BANK + hi],
+                        in_=rows[:, (n - 1) * width : (n + 1) * width].rearrange("p (n m) -> p n m", n=2),
+                    )
 
-        for index, piece in enumerate(PIECES):
-            update(last, *piece)
-            pair_up(*piece)
-            weave_words(*piece)
-            quantise_piece(*piece)
-            scores(index, *piece)
+        for c, lo, hi in PIECES:
+            update(SLICES - 1, c, lo, hi)
+            pair_up(c, lo, hi)
+            weave_words(c, lo, hi)
+            piece_codes = keep.tile([P, hi - lo], U32, name=f"codes_z{c}_{lo}", align_bytes=64)
+            quantise(("z", 1, c, lo), piece_codes[:], hi - lo)
+            scores(c, lo, hi, shared=(c, lo, hi) == PIECES[-1])

from contextlib import ExitStack

import concourse.mybir as mybir
from concourse.masks import make_identity

K, T, S, T2, H, N = 1024, 2048, 1024, 2048, 1024, 512
FLOPS = 2 * K * H * S + 2 * H * N * T2

F32 = mybir.dt.float32
BF16 = mybir.dt.bfloat16
I32 = mybir.dt.int32
U32 = mybir.dt.uint32
U16 = mybir.dt.uint16
U8 = mybir.dt.uint8
FP8X4 = mybir.dt.float8_e4m3fn_x4
FP4X4 = mybir.dt.float4_e2m1fn_x4
ALU = mybir.AluOpType
ACT = mybir.ActivationFunctionType

P = 128
PACK = 4
PASSES = 2
BANK = 512
QUADS = 4
RUN = 4
SLICES = PASSES * PACK
CHUNKS = T2 // BANK
STEPS = T2 // (2 * P)

PAGE_OF = (0, 1, 2, 3, 0, 1, 2, 2)
CAL_SLOT = ("wide2", "wide3", "wide0", "wide1", "wide4", "wide5", "wide6", "wide1")
DAMP_SLOT = ("damp0", "damp1", "damp2", "damp0", "damp1", "wide2", "wide3", "wide0")
PICKED_SLOT = ("wide0", "wide1", "wide4", "wide5")
STAGE_SLOT = ("wide4", "wide5", "wide2", "rows1")
PIECES = ((0, 0, 256), (0, 256, 512), (1, 0, 512), (2, 0, 512), (3, 0, 512))
PRED_BANKS = (0, 1)
ALL_BANKS = (2, 3, 4, 5, 6, 7, 0, 1)


def tile_list_axle_calibration_audit_kernel(
    tc, tab_words, tab_scales, offs, w1_words, w1_scales, reads, gain, offs2, wgs, cal, w2, out
):
    nc = tc.nc
    with ExitStack() as ctx:
        keep = ctx.enter_context(tc.tile_pool(name="keep", bufs=1))
        ring = ctx.enter_context(tc.tile_pool(name="ring", bufs=3))
        psum = ctx.enter_context(tc.psum_pool(name="psum", bufs=1))
        uses = {}

        def next_bank(banks):
            n = uses.get(banks, 0)
            uses[banks] = n + 1
            return psum.tile([P, BANK], F32, name="bank", tag=f"bank{banks[n % len(banks)]}")

        pick = keep.tile([P, S // 16], U16, name="pick")
        place = keep.tile([P, S // 16], U16, name="place")

        w1_sc_raw = keep.tile([P, PASSES, H], U8, name="w1_sc_raw", tag="rows1", align_bytes=64)
        warm = keep.tile([P, 2], F32, name="warm")
        v_s = keep.tile([P, PASSES, S], U8, name="v_s", align_bytes=64)
        nc.gpsimd.memset(w1_sc_raw[:].bitcast(I32), 0)
        nc.gpsimd.memset(warm[:, 0:1], 1.0)
        nc.gpsimd.memset(v_s[:].bitcast(I32), 0)
        nc.sync.dma_start(pick[:], offs)
        tab_sc = keep.tile([P, T], U8, name="tab_sc", tag="damp0", align_bytes=64)
        nc.sync.dma_start(
            out=tab_sc[:].bitcast(I32),
            in_=tab_scales.rearrange("a q n -> (a q) n").bitcast(I32).unsqueeze(0).broadcast_to([QUADS, 32, T // 4]),
        )
        nc.sync.dma_start(place[:], offs2)
        gain_t = keep.tile([P, PASSES, PACK], F32, name="gain_t")
        nc.sync.dma_start(out=gain_t[:], in_=gain.rearrange("(b p i) -> p b i", b=PASSES, i=PACK))
        w1_raw = keep.tile([P, PASSES, 2 * H], U8, name="w1_raw", tag="wgs", align_bytes=64)
        nc.sync.dma_start(out=w1_raw[:].bitcast(I32), in_=w1_words.rearrange("a p n -> p a n").bitcast(I32))
        tab_w = [keep.tile([P, T], I32, name=f"tab_w{a}", tag=f"late{a}", align_bytes=64) for a in range(PASSES)]
        for a in range(PASSES):
            nc.sync.dma_start(out=tab_w[a][:], in_=tab_words[a].rearrange("p t i -> p (t i)").bitcast(I32))
        for q in range(QUADS):
            nc.scalar.dma_start(
                out=w1_sc_raw[32 * q : 32 * q + 4].bitcast(I32),
                in_=w1_scales[:, 4 * q : 4 * q + 4, :].rearrange("a r n -> r a n").bitcast(I32),
            )
        nc.scalar.activation(out=warm[:, 1:2], in_=warm[:, 0:1], func=ACT.Abs_reciprocal_sqrt, bias=1.0)
        picked_sc = keep.tile([P, S], U8, name="picked_sc", tag="rows4", align_bytes=64)
        nc.vector.tensor_copy(out=picked_sc[:], in_=tab_sc[:].indirect(pick[:]))
        for a in range(PASSES):
            for q in range(QUADS):
                row = 32 * q + 16 * a + 4 * q
                nc.scalar.dma_start(
                    out=v_s[32 * q : 32 * q + 4, a, :].bitcast(I32), in_=picked_sc[row : row + 4, :].bitcast(I32)
                )
        ident = keep.tile([P, P], F32, name="ident")
        make_identity(nc, ident[:])

        reads_v = reads.rearrange("(b p i) j -> b p (i j)", b=PASSES, i=PACK)
        cal_v = cal.rearrange("(b p i) m -> b i p m", b=PASSES, i=PACK)
        resid = {}
        cal_t = {}

        def load_reads(first, count):
            b, i = divmod(first, PACK)
            rows = keep.tile([P, count * S], F32, name="rows", tag=f"rows{first}", align_bytes=64)
            nc.sync.dma_start(out=rows[:], in_=reads_v[b][:, i * S : (i + count) * S])
            for s in range(count):
                resid[first + s] = rows[:, s * S : (s + 1) * S]

        def load_cal(s):
            cal_t[s] = keep.tile([P, T2], F32, name="cal_s", tag=CAL_SLOT[s], align_bytes=64)
            nc.sync.dma_start(out=cal_t[s][:], in_=cal_v[s // PACK, s % PACK])

        load_reads(0, 1)

        pages = [keep.tile([P, T2], F32, name=f"page{u}") for u in range(2)]
        for page in pages:
            nc.vector.memset(page[:], 0.0)

        w1_c = [
            keep.tile([P, PASSES, PACK, 2 * P], U8, name=f"w1_c{b}", tag=("wide2", "wide6")[b], align_bytes=64)
            for b in range(PASSES)
        ]
        w1_s = [
            keep.tile([P, PASSES, PACK, P], U8, name=f"w1_s{b}", tag=("wide3", "w1_s")[b], align_bytes=64)
            for b in range(PASSES)
        ]

        def order_w1(b):
            cols = slice(b * BANK, (b + 1) * BANK)
            nc.vector.tensor_copy(
                out=w1_c[b][:].bitcast(U16),
                in_=w1_raw[:].bitcast(U16)[:, :, cols].rearrange("p a (m i) -> p a i m", i=PACK),
            )
            nc.vector.tensor_copy(
                out=w1_s[b][:], in_=w1_sc_raw[:, :, cols].rearrange("p a (m i) -> p a i m", i=PACK)
            )

        v_w = {}

        def gather(h):
            entries = pick[:, h * (BANK // 16) : (h + 1) * (BANK // 16)]
            for a in range(PASSES):
                v_w[a, h] = keep.tile([P, BANK], U32, name=f"v_w{a}{h}", tag=PICKED_SLOT[a + 2 * h], align_bytes=64)
                nc.vector.tensor_copy(out=v_w[a, h][:], in_=tab_w[a][:].bitcast(U32).indirect(entries))

        def residual(s, h):
            b, i = divmod(s, PACK)
            cols = slice(h * BANK, (h + 1) * BANK)
            acc = next_bank(PRED_BANKS)
            for a in range(PASSES):
                nc.tensor.matmul_mx(
                    out=acc[:],
                    lhsT=w1_c[b][:, a, i, :].bitcast(FP4X4),
                    lhsT_scale=w1_s[b][:, a, i, :],
                    rhs=v_w[a, h][:].bitcast(FP8X4),
                    rhs_scale=v_s[:, a, cols],
                    start=(a == 0),
                    stop=(a == PASSES - 1),
                )
            nc.vector.tensor_tensor(out=resid[s][:, cols], in0=resid[s][:, cols], in1=acc[:], op=ALU.subtract)

        damping = {}

        def damp(s, cols):
            b, i = divmod(s, PACK)
            if s not in damping:
                damping[s] = keep.tile([P, S], F32, name="damping", tag=DAMP_SLOT[s], align_bytes=64)
            d, f = resid[s][:, cols], damping[s][:, cols]
            nc.scalar.activation(out=f, in_=d, func=ACT.Square)
            nc.scalar.activation(out=f, in_=f, func=ACT.Abs_reciprocal_sqrt, bias=1.0)
            nc.scalar.activation(out=f, in_=f, func=ACT.Square)
            nc.vector.scalar_tensor_tensor(
                out=d, in0=d, scalar=gain_t[:, b, i : i + 1], in1=wgs_t[:, cols], op0=ALU.mult, op1=ALU.mult
            )

        def put(s, cols):
            window = pages[PAGE_OF[s]][:].indirect(place[:, cols.start // 16 : cols.stop // 16])
            nc.vector.tensor_tensor(out=window, in0=resid[s][:, cols], in1=damping[s][:, cols], op=ALU.mult)

        turned = {}

        def turn_step(pair, q):
            acc = next_bank(ALL_BANKS)
            for mb in range(2):
                cols = slice((2 * q + mb) * P, (2 * q + mb + 1) * P)
                for e in range(2):
                    s = 2 * pair + e
                    dst = acc[:, (2 * mb + e) * P : (2 * mb + e + 1) * P]
                    nc.tensor.matmul(dst, cal_t[s][:, cols], ident[:], start=True, stop=False, is_transpose=True)
                    nc.tensor.matmul(
                        dst, pages[PAGE_OF[s]][:, cols], ident[:], start=False, stop=True, is_transpose=True
                    )
            if q == 0:
                turned[pair] = keep.tile([P, STEPS * BANK], BF16, name="turned", tag=f"turned{pair}", align_bytes=64)
            turned[pair, q] = turned[pair][:, q * BANK : (q + 1) * BANK]
            nc.scalar.copy(
                out=turned[pair, q].rearrange("m (b p e) -> m b p e", b=2, e=2),
                in_=acc[:].rearrange("m (b e p) -> m b p e", b=2, e=2),
            )

        def turn(pair):
            for q in range(STEPS):
                turn_step(pair, q)

        woven = {}

        def new_woven(key):
            if key[:2] == ("z", 0):
                woven[key] = keep.tile([P, BANK * PACK], BF16, name="woven0", tag=f"z_rows{key[2]}", align_bytes=64)
            else:
                woven[key] = ring.tile([P, BANK * PACK], BF16, name="woven", tag="woven", align_bytes=64)

        def turn_back_woven(q):
            key = ("z", 0, q // 2)
            if key not in woven:
                new_woven(key)
            acc = next_bank(ALL_BANKS)
            for u in range(2):
                words = turned[u, q].bitcast(F32)
                for mb in range(2):
                    nc.tensor.transpose(
                        acc[:, (2 * u + mb) * P : (2 * u + mb + 1) * P], words[:, mb * P : (mb + 1) * P], ident[:]
                    )
            dst = woven[key][:].bitcast(F32)[:, (q % 2) * BANK : (q % 2 + 1) * BANK]
            nc.scalar.copy(out=dst.rearrange("p (m u) -> p m u", u=2), in_=acc[:].rearrange("p (u m) -> p m u", u=2))

        pair_words = {}
        z_rows = {}

        def turn_back_words(c):
            if c % 2 == 0:
                both = keep.tile([P, 4 * BANK], F32, name="pair_words", tag=f"turned{c // 2}", align_bytes=64)
                pair_words[c] = both[:, 0 : 2 * BANK]
                pair_words[c + 1] = both[:, 2 * BANK : 4 * BANK]
            acc = next_bank(ALL_BANKS)
            for blk in range(BANK // P):
                words = turned[2, 2 * c + blk // 2].bitcast(F32)
                nc.tensor.transpose(
                    acc[:, blk * P : (blk + 1) * P], words[:, (blk % 2) * P : (blk % 2 + 1) * P], ident[:]
                )
            nc.scalar.copy(out=pair_words[c][:, 0:BANK], in_=acc[:])

        def update(s, c, lo, hi):
            cols = slice(c * BANK + lo, c * BANK + hi)
            e = s % 2
            if c not in z_rows:
                z_rows[c] = keep.tile([P, 2 * BANK], BF16, name="z_rows", tag=f"z_rows{c}", align_bytes=64)
            nc.vector.tensor_tensor(
                out=z_rows[c][:, e * BANK + lo : e * BANK + hi],
                in0=cal_t[s][:, cols],
                in1=pages[PAGE_OF[s]][:, cols],
                op=ALU.add,
            )

        def pair_up(c, lo, hi):
            rows = z_rows[c][:].rearrange("p (e m) -> p e m", e=2)[:, :, lo:hi]
            nc.vector.tensor_copy(
                out=pair_words[c][:, BANK + lo : BANK + hi].bitcast(BF16).rearrange("p (k j e) -> p k e j", j=RUN, e=2),
                in_=rows.rearrange("p e (k j) -> p k e j", j=RUN),
            )

        def weave_words(c, lo, hi):
            key = ("z", 1, c, lo)
            new_woven(key)
            rows = pair_words[c].rearrange("p (u m) -> p u m", u=2)[:, :, lo:hi]
            nc.vector.tensor_copy(
                out=woven[key][:, 0 : (hi - lo) * PACK].bitcast(F32).rearrange("p (k j u) -> p k u j", j=RUN, u=2),
                in_=rows.rearrange("p u (k j) -> p k u j", j=RUN),
            )

        codes, scales = {}, {}

        def quantise(key, dst, width):
            codes[key] = dst
            scales[key] = keep.tile([P, width], U8, name="scales_" + "_".join(map(str, key)), align_bytes=64)
            nc.vector.quantize_mx(out=dst.bitcast(FP8X4), scales=scales[key][:], in_=woven[key][:, 0 : width * PACK])

        def weave_w2(b):
            raw = keep.tile([P, PACK, N], F32, name="w2_raw", tag=f"wide{b}", align_bytes=64)
            nc.sync.dma_start(out=raw[:], in_=w2[b * BANK : (b + 1) * BANK, :].rearrange("(p i) n -> p i n", i=PACK))
            key = ("w", b)
            new_woven(key)
            nc.scalar.copy(
                out=woven[key][:].rearrange("p (k j t) -> p k t j", j=RUN, t=PACK),
                in_=raw[:].rearrange("p t (k j) -> p k t j", j=RUN),
            )

        whole = slice(0, S)
        halves = [slice(0, BANK), slice(BANK, S)]

        order_w1(0)
        order_w1(1)
        wgs_t = keep.tile([P, S], F32, name="wgs_t", tag="wgs", align_bytes=64)
        nc.scalar.dma_start(out=wgs_t[:], in_=wgs)
        load_reads(1, PACK - 1)
        load_reads(PACK, PACK)
        for h in range(2):
            gather(h)
            residual(0, h)
            damp(0, halves[h])
        for s in range(1, SLICES):
            residual(s, 0)
            residual(s, 1)
            if s < 3:
                damp(s, whole)
            if s == PACK - 1:
                load_cal(0)
                load_cal(1)
        weave_w2(0)
        weave_w2(1)
        for s in range(2, SLICES - 1):
            load_cal(s)
        for a in range(PASSES):
            page = keep.tile([P, T2], F32, name=f"page{2 + a}", tag=f"late{a}", align_bytes=64)
            nc.vector.memset(page[:], 0.0)
            pages.append(page)

        put(0, halves[0])
        put(0, halves[1])
        damp(3, whole)
        put(1, whole)
        damp(4, whole)
        turn(0)
        damp(5, whole)
        damp(6, whole)
        put(2, whole)
        put(3, whole)
        turn(1)
        damp(7, whole)
        load_cal(7)
        for q in range(STEPS):
            turn_back_woven(q)
        put(4, whole)
        w2_codes = keep.tile([P, PASSES * N], U32, name="w2_codes", tag=DAMP_SLOT[4], align_bytes=64)
        for b in range(PASSES):
            quantise(("w", b), w2_codes[:, b * N : (b + 1) * N], N)
        put(5, whole)
        for q in range(STEPS):
            turn_step(2, q)
            if q >= 2 and q % 2 == 0:
                turn_back_words(q // 2 - 1)
        turn_back_words(CHUNKS - 1)
        put(6, whole)
        z_codes = keep.tile([P, T2], U32, name="z_codes", tag=DAMP_SLOT[6], align_bytes=64)
        for c in range(CHUNKS):
            quantise(("z", 0, c), z_codes[:, c * BANK : (c + 1) * BANK], BANK)
        for c in range(CHUNKS):
            update(6, c, 0, BANK)
        put(7, whole)

        staged = [keep.tile([P, T2], F32, name="staged", tag=tag, align_bytes=64) for tag in STAGE_SLOT]
        out_v = out.rearrange("(n p) m -> p n m", p=P)

        def scores(c, lo, hi, shared):
            width = hi - lo
            rows = staged[c][:, (N // P) * lo : (N // P) * hi]
            moving = (
                (codes["z", 0, c][:, lo:hi], scales["z", 0, c][:, lo:hi]),
                (codes["z", 1, c, lo], scales["z", 1, c, lo][:]),
            )
            for n in range(N // P):
                acc = next_bank(ALL_BANKS)
                for b in range(PASSES):
                    nc.tensor.matmul_mx(
                        out=acc[:, 0:width],
                        lhsT=codes["w", b][:, n * P : (n + 1) * P].bitcast(FP8X4),
                        lhsT_scale=scales["w", b][:, n * P : (n + 1) * P],
                        rhs=moving[b][0].bitcast(FP8X4),
                        rhs_scale=moving[b][1],
                        start=(b == 0),
                        stop=(b == PASSES - 1),
                    )
                res = rows[:, n * width : (n + 1) * width]
                if shared and n % 2 == 1:
                    nc.vector.tensor_copy(out=res, in_=acc[:, 0:width])
                else:
                    nc.scalar.copy(out=res, in_=acc[:, 0:width])
                if n % 2 == 1:
                    nc.sync.dma_start(
                        out=out_v[:, n - 1 : n + 1, c * BANK + lo : c * BANK + hi],
                        in_=rows[:, (n - 1) * width : (n + 1) * width].rearrange("p (n m) -> p n m", n=2),
                    )

        for c, lo, hi in PIECES:
            update(SLICES - 1, c, lo, hi)
            pair_up(c, lo, hi)
            weave_words(c, lo, hi)
            piece_codes = keep.tile([P, hi - lo], U32, name=f"codes_z{c}_{lo}", align_bytes=64)
            quantise(("z", 1, c, lo), piece_codes[:], hi - lo)
            scores(c, lo, hi, shared=(c, lo, hi) == PIECES[-1])
